import numpy as np
import ml_dtypes


def mxq(x, axis, fmt="e4m3"):
    dtype, down = {"e4m3": (ml_dtypes.float8_e4m3fn, 7), "e5m2": (ml_dtypes.float8_e5m2, 14)}[fmt]
    v = np.moveaxis(np.asarray(x, np.float32).astype(ml_dtypes.bfloat16).astype(np.float64), axis, -1)
    blocks = v.reshape(v.shape[:-1] + (-1, 32))
    amax = np.abs(blocks).max(-1, keepdims=True)
    byte = np.maximum(np.where(amax > 0, np.frexp(amax)[1] - 1 + 127, 0) - down, 1)
    scale = np.exp2(byte - 127.0)
    codes = (blocks / scale).astype(np.float32).astype(dtype).astype(np.float64)
    return np.moveaxis((codes * scale).reshape(v.shape), -1, axis)


WIDE = False


def mx_kscale(k):
    if not WIDE:
        return np.ones(k)
    levels = np.array([10, -10, 5, -5, 0])
    if k % 512:
        return np.exp2(np.random.permutation(np.resize(levels, k // 32))).repeat(32)
    a = np.empty((k // 512, 16))
    for p in range(k // 512):
        a[p, :8] = np.random.permutation(np.resize(levels, 8))
        for g in range(8):
            far = levels[np.abs(levels - a[p, g]) >= 10]
            a[p, g + 8] = far[np.random.randint(len(far))]
    return np.exp2(a.ravel()).repeat(32)


def f64(x):
    return np.asarray(x).astype(np.float64)


def striped(idx):
    return np.tile(idx.reshape(-1, 16).T, (8, 1)).astype(np.uint16)


def unstriped(offs):
    return offs[:16].T.reshape(-1).astype(np.int64)


def striped8(idx):
    return np.concatenate([x.reshape(-1, 16).T for x in idx]).astype(np.uint16)


def runs(offs, k):
    lists = np.stack([offs[16 * r : 16 * r + 16].T.reshape(-1) for r in range(8)]).astype(np.int64)
    return lists[np.arange(k) % 512 // 64]


def pack_weight(w):
    k, n = w.shape
    w = f64(np.asarray(w, np.float32).astype(ml_dtypes.bfloat16)).reshape(k // 32, 32, n)
    amax = np.abs(w).max(1)
    byte = np.clip(np.where(amax > 0, np.frexp(amax)[1] - 1 + 127 - 7, 1), 1, 254)
    scaled = (w * np.exp2(127.0 - byte)[:, None, :]).reshape(k, n).astype(np.float32)
    words = np.ascontiguousarray(scaled.reshape(k // 512, 128, 4, n).transpose(0, 1, 3, 2)).astype(ml_dtypes.float8_e4m3fn).view(np.uint8)
    return words, np.ascontiguousarray(byte.astype(np.uint8).reshape(k // 512, 16, n))


def unpack_weight(words, scales):
    g, p, n, _ = words.shape
    vals = np.ascontiguousarray(words).view(ml_dtypes.float8_e4m3fn).astype(np.float64) * np.repeat(np.exp2(scales.astype(np.float64) - 127.0), 8, axis=1)[..., None]
    return vals.transpose(0, 1, 3, 2).reshape(g * 512, n)


def relu(v):
    return np.maximum(v, 0.0)

def planes(y):
    n, m = y.shape
    v = y.astype(np.float32).astype(ml_dtypes.bfloat16).astype(np.float64).reshape(n // 32, 32, m)
    top = np.abs(v).max(1)
    byte = np.clip(np.where(top > 0, np.frexp(top)[1] - 1 + 127 - 7, 1), 1, 254)
    codes = (v * np.exp2(127.0 - byte)[:, None, :]).reshape(n, m).astype(np.float32).astype(ml_dtypes.float8_e4m3fn).view(np.uint8)
    words = codes.reshape(n // 512, 128, 4, m).transpose(0, 1, 3, 2)
    return np.ascontiguousarray(words), np.ascontiguousarray(byte.astype(np.uint8).reshape(n // 512, 16, m))


K, T, S, N, H, W, U = 512, 2048, 512, 512, 512, 256, 1024


def setup_inputs():
    n = np.random.standard_normal
    s = mx_kscale(K)[:, None]
    u = mx_kscale(S)
    packed_xT = pack_weight(n((K, T)) * s)
    perm = np.stack([np.random.permutation(H) for _ in range(8)])
    return {
        "x_words": packed_xT[0],
        "x_scales": packed_xT[1],
        "wa": (n((K, H)) / np.sqrt(K) / s).astype(np.float32),
        "wb": (n((K, N)) / np.sqrt(K) / s).astype(np.float32),
        "gt": (np.random.uniform(0.5, 1.5, (S, 1)) * u[:, None]).astype(np.float32),
        "gi": (np.random.uniform(0.5, 1.5, (S, 1)) / u[:, None]).astype(np.float32),
        "offs": striped(np.random.permutation(T)[:S]),
        "two": striped(np.random.permutation(T)[:S]),
        "n1": striped8(perm[:, :W]),
        "n2": striped8(perm[:, W:]),
        "n3": striped8(np.stack([np.random.permutation(U)[:N] for _ in range(8)])),
        "n4": striped8(np.stack([np.random.permutation(N) for _ in range(8)])),
    }


def reference(x_words, x_scales, wa, wb, gt, gi, offs, two, n1, n2, n3, n4):
    xq = unpack_weight(x_words, x_scales)[:, unstriped(offs)]
    a = xq.T @ mxq(f64(wa), 0, "e4m3")
    pa = a[np.arange(S)[:, None], runs(n1, S)]
    pb = a[np.arange(S)[:, None], runs(n2, S)]
    rb = np.minimum(pa, pb)
    ra = np.maximum(pa, pb)
    ds = np.zeros((S, H))
    ds[np.arange(S)[:, None], runs(n1, S)] = ra
    dt = ds.copy()
    dt[np.arange(S)[:, None], runs(n2, S)] = rb
    z = f64(gt) * dt
    x_two = unpack_weight(x_words, x_scales)[:, unstriped(two)]
    b = x_two.T @ mxq(f64(wb), 0, "e4m3")
    z2 = f64(gi) * b
    cv = 0.0625 * ((mxq(z, 0, "e4m3").T @ mxq(z2, 0, "e4m3")))
    nw = cv - (relu(cv[np.arange(H)[:, None], runs(n4, H)]))
    out = np.zeros((H, U))
    out[np.arange(H)[:, None], runs(n3, H)] = nw
    return (out,) + planes(out)

@@ -1,0 +1,264 @@
+from contextlib import ExitStack
+
+import concourse.mybir as mybir
+from concourse.masks import make_identity
+
+K, T, S, N, H, W, U = 512, 2048, 512, 512, 512, 256, 1024
+FLOPS = 2 * K * S * H + 2 * K * S * N + 2 * S * H * N
+
+F32 = mybir.dt.float32
+BF16 = mybir.dt.bfloat16
+I32 = mybir.dt.int32
+U32 = mybir.dt.uint32
+U16 = mybir.dt.uint16
+U8 = mybir.dt.uint8
+FP8X4 = mybir.dt.float8_e4m3fn_x4
+ALU = mybir.AluOpType
+ACT = mybir.ActivationFunctionType
+
+P = 128
+PACK = 4
+BLOCKS = 16
+RUN = 8
+VECTOR_COLS = 640
+QCOLS = 256
+
+
+def tile_picked_momorderpagez_none_po_kernel(
+    tc, x_words, x_scales, wa, wb, gt, gi, offs, two, n1, n2, n3, n4, out_0, out_1, out_2
+):
+    nc = tc.nc
+    with ExitStack() as ctx:
+        keep = ctx.enter_context(tc.tile_pool(name="keep", bufs=1))
+        banks = ctx.enter_context(tc.psum_pool(name="banks", bufs=7))
+        turn = ctx.enter_context(tc.psum_pool(name="turn", bufs=1))
+
+        def sb(name, shape, dtype):
+            return keep.tile(shape, dtype, name=name, align_bytes=64)
+
+        def load_list(name, src):
+            t = sb(name, list(src.shape), U16)
+            nc.sync.dma_start(t[:], src)
+            return t
+
+        xs = sb("xs", [P, T], U8)
+        nc.vector.memset(xs[:].bitcast(I32), 0)
+        l_offs = load_list("l_offs", offs)
+        xw = sb("xw", [P, T], I32)
+        nc.sync.dma_start(xw[:], x_words[0].rearrange("p c r -> p (c r)").bitcast(I32))
+        for q in range(4):
+            nc.scalar.dma_start(xs[32 * q : 32 * q + 4, :].bitcast(I32), x_scales[0, 4 * q : 4 * q + 4, :].bitcast(I32))
+        wa_raw = [sb("wa_raw%d" % h, [P, PACK, H // 2], F32) for h in range(2)]
+        for h in range(2):
+            nc.sync.dma_start(wa_raw[h][:], wa.rearrange("(p j) c -> p j c", j=PACK)[:, :, h * 256 : (h + 1) * 256])
+        l_two = load_list("l_two", two)
+        l_n1 = load_list("l_n1", n1)
+        l_n2 = load_list("l_n2", n2)
+        wb_raw = sb("wb_raw", [P, PACK, N], F32)
+        nc.sync.dma_start(wb_raw[:], wb.rearrange("(p j) c -> p j c", j=PACK))
+        l_n4 = load_list("l_n4", n4)
+        l_n3 = load_list("l_n3", n3)
+
+        rows = sb("rows", [P, P], F32)
+        nc.gpsimd.memset(rows[:], 0.0)
+        for i, vec in enumerate((gt, gi)):
+            nc.gpsimd.dma_start(
+                rows[4 * i : 4 * i + 4, :].rearrange("t (b j) -> t b j", j=RUN),
+                vec.rearrange("(b t j) o -> t b (j o)", t=PACK, j=RUN),
+            )
+        ident = sb("ident", [P, P], F32)
+        make_identity(nc, ident[:])
+
+        pages = [sb("page%d" % t, [P, U], F32) for t in range(PACK)]
+        for t in range(PACK):
+            nc.vector.memset(pages[t][:], 0.0)
+
+        turned = turn.tile([P, P], F32, name="turned")
+        nc.tensor.transpose(turned[:], rows[:], ident[:])
+        gt_abs = sb("gt_abs", [P, PACK], F32)
+        gt_sign = sb("gt_sign", [P, PACK], F32)
+        gi_sb = sb("gi_sb", [P, PACK], F32)
+        gi_signed = sb("gi_signed", [P, PACK], F32)
+        nc.scalar.activation(gt_abs[:], turned[:, 0:4], ACT.Abs)
+        nc.scalar.activation(gt_sign[:], turned[:, 0:4], ACT.Sign)
+        nc.scalar.copy(gi_sb[:], turned[:, 4:8])
+        nc.gpsimd.tensor_tensor(gi_signed[:], gi_sb[:], gt_sign[:], ALU.mult)
+
+        def gather_words(name, lst):
+            g = sb(name, [P, S], U32)
+            nc.vector.tensor_copy(
+                g[:].rearrange("p (t b j) -> p b t j", t=PACK, j=RUN), xw[:].bitcast(U32).indirect(lst[:])
+            )
+            return g
+
+        def gather_bytes(name, lst):
+            g = sb(name, [P, S], U8)
+            nc.vector.tensor_copy(g[:], xs[:].indirect(lst[:]))
+            return g
+
+        def deal_bytes(name, g):
+            d = sb(name, [P, S], U8)
+            nc.vector.tensor_copy(
+                d[:].bitcast(I32).rearrange("p (t b w) -> p t b w", t=PACK, w=2),
+                g[:].bitcast(I32).rearrange("p (b t w) -> p t b w", t=PACK, w=2),
+            )
+            return d
+
+        def round_weights(dst, raw):
+            nc.scalar.copy(
+                dst.rearrange("p (c i t) -> p c t i", i=4, t=PACK), raw.rearrange("p t (c i) -> p c t i", i=4)
+            )
+
+        def quantize(codes, scales, src):
+            nc.vector.quantize_mx(out=codes.bitcast(FP8X4), scales=scales, in_=src)
+
+        def product(lc, ls, rc, rs, t):
+            acc = banks.tile([P, 512], F32, name="acc")
+            cols = slice(t * P, (t + 1) * P)
+            nc.tensor.matmul_mx(
+                out=acc[:], lhsT=lc[:, cols].bitcast(FP8X4), lhsT_scale=ls[:, cols],
+                rhs=rc[:].bitcast(FP8X4), rhs_scale=rs[:], start=True, stop=True,
+            )
+            return acc
+
+        xa_words = gather_words("xa_words", l_offs)
+        xa_raw = gather_bytes("xa_raw", l_offs)
+        xb_words = gather_words("xb_words", l_two)
+        xa_scales = deal_bytes("xa_scales", xa_raw)
+
+        wa_bf = sb("wa_bf", [P, H * PACK], BF16)
+        wa_codes = sb("wa_codes", [P, H], U32)
+        wa_scales = sb("wa_scales", [P, H], U8)
+        for h in range(2):
+            round_weights(wa_bf[:, h * 1024 : (h + 1) * 1024], wa_raw[h][:])
+        quantize(wa_codes[:], wa_scales[:], wa_bf[:])
+
+        xb_raw = gather_bytes("xb_raw", l_two)
+        xb_scales = deal_bytes("xb_scales", xb_raw)
+
+        a = [sb("a%d" % t, [P, H], F32) for t in range(PACK)]
+        for t in range(PACK):
+            acc = product(xa_words, xa_scales, wa_codes, wa_scales, t)
+            nc.scalar.activation(a[t][:], acc[:], ACT.Copy, scale=gt_abs[:, t : t + 1])
+
+        wb_bf = sb("wb_bf", [P, N * PACK], BF16)
+        wb_codes = sb("wb_codes", [P, N], U32)
+        wb_scales = sb("wb_scales", [P, N], U8)
+        round_weights(wb_bf[:], wb_raw[:])
+
+        pa = sb("pa", [P, PACK * W], F32)
+        pb = sb("pb", [P, PACK * W], F32)
+        ra = sb("ra", [P, PACK * W], F32)
+        rb = sb("rb", [P, PACK * W], F32)
+        for t in range(PACK):
+            nc.vector.tensor_copy(pa[:, t * W : (t + 1) * W], a[t][:].indirect(l_n1[:]))
+            nc.vector.tensor_copy(pb[:, t * W : (t + 1) * W], a[t][:].indirect(l_n2[:]))
+        quantize(wb_codes[:], wb_scales[:], wb_bf[:])
+        nc.vector.tensor_tensor(ra[:], pa[:], pb[:], ALU.max)
+        nc.vector.tensor_tensor(rb[:], pa[:], pb[:], ALU.min)
+
+        z2_bf = sb("z2_bf", [P, N * PACK], BF16)
+        z2_view = z2_bf[:].rearrange("p (c t) -> p c t", t=PACK)
+        for t in range(PACK):
+            acc = product(xb_words, xb_scales, wb_codes, wb_scales, t)
+            nc.scalar.activation(z2_view[:, :, t], acc[:], ACT.Copy, scale=gi_signed[:, t : t + 1])
+
+        dt = [sb("dt%d" % t, [P, H], F32) for t in range(PACK)]
+        z_bf = sb("z_bf", [P, H * PACK], BF16)
+        z_view = z_bf[:].rearrange("p (u m t) -> p m u t", u=PACK, t=PACK)
+        z_codes = sb("z_codes", [P, H], U32)
+        z_scales = sb("z_scales", [P, H], U8)
+        z2_codes = sb("z2_codes", [P, N], U32)
+        z2_scales = sb("z2_scales", [P, N], U8)
+
+        def put_larger(t):
+            nc.vector.tensor_copy(dt[t][:].indirect(l_n1[:]), ra[:, t * W : (t + 1) * W])
+
+        def put_smaller(t):
+            nc.vector.tensor_copy(dt[t][:].indirect(l_n2[:]), rb[:, t * W : (t + 1) * W])
+
+        def round_z(t):
+            src = dt[t][:].rearrange("p (m u) -> p m u", u=PACK)
+            if t == 2:
+                nc.scalar.copy(z_view[:, :, :, 2:4], src.unsqueeze(3).to_broadcast([P, P, PACK, 2]))
+            else:
+                nc.scalar.copy(z_view[:, :, :, t], src)
+
+        put_larger(0)
+        for t in range(PACK - 1):
+            put_larger(t + 1)
+            put_smaller(t)
+            round_z(t)
+        quantize(z2_codes[:], z2_scales[:], z2_bf[:])
+        put_smaller(3)
+
+        last = dt[3][:].rearrange("p (m u) -> p m u", u=PACK)
+
+        def round_last(u):
+            nc.vector.tensor_copy(z_view[:, :, u, 3], last[:, :, u])
+
+        def quantize_z(u):
+            quantize(z_codes[:, u * P : (u + 1) * P], z_scales[:, u * P : (u + 1) * P], z_bf[:, u * 512 : (u + 1) * 512])
+
+        round_last(0)
+        for u in range(PACK):
+            if u + 1 < PACK:
+                round_last(u + 1)
+            quantize_z(u)
+
+        cv = [sb("cv%d" % u, [P, N], F32) for u in range(PACK)]
+        pos = [sb("pos%d" % u, [P, N], F32) for u in range(PACK)]
+        neg = [sb("neg%d" % u, [P, N], F32) for u in range(PACK)]
+        for u in range(PACK):
+            acc = product(z_codes, z_scales, z2_codes, z2_scales, u)
+            nc.scalar.activation(pos[u][:], acc[:], ACT.Relu, scale=0.0625)
+            nc.scalar.activation(cv[u][:], acc[:], ACT.Copy, scale=0.0625)
+
+        page_bf = sb("page_bf", [P, U * PACK], BF16)
+        page_view = page_bf[:].rearrange("p (c t) -> p c t", t=PACK)
+        out_rows = out_0.rearrange("(p t) c -> p t c", t=PACK)
+
+        def fetch(u):
+            for h in range(2):
+                nc.vector.tensor_scalar(
+                    neg[u][:, h * W : (h + 1) * W], pos[u][:].indirect(l_n4[:, h * 16 : (h + 1) * 16]),
+                    -1.0, 0.0, ALU.mult, ALU.add,
+                )
+
+        def put_page(u):
+            nc.vector.tensor_tensor(pages[u][:].indirect(l_n3[:]), cv[u][:], neg[u][:], ALU.add)
+            nc.sync.dma_start(out_rows[:, u, :], pages[u][:])
+
+        fetch(0)
+        for u in range(PACK - 1):
+            fetch(u + 1)
+            put_page(u)
+            if u == 2:
+                nc.scalar.copy(page_view[:, :, 2:4], pages[u][:].unsqueeze(2).to_broadcast([P, U, 2]))
+            else:
+                nc.scalar.copy(page_view[:, :, u], pages[u][:])
+        put_page(3)
+
+        o_codes = sb("o_codes", [P, U], U32)
+        o_scales = sb("o_scales", [P, U], U8)
+        words_out = out_1[0].rearrange("p c r -> p (c r)").bitcast(I32)
+
+        def round_page(engine_copy, c0, c1):
+            engine_copy(page_view[:, c0:c1, 3], pages[3][:, c0:c1])
+
+        def finish(i):
+            cols = slice(i * QCOLS, (i + 1) * QCOLS)
+            quantize(o_codes[:, cols], o_scales[:, cols], page_bf[:, i * QCOLS * PACK : (i + 1) * QCOLS * PACK])
+            nc.sync.dma_start(words_out[:, cols], o_codes[:, cols].bitcast(I32))
+
+        round_page(nc.scalar.copy, VECTOR_COLS, 3 * QCOLS)
+        round_page(nc.scalar.copy, 3 * QCOLS, U)
+        round_page(nc.vector.tensor_copy, 0, QCOLS)
+        round_page(nc.vector.tensor_copy, QCOLS, 2 * QCOLS)
+        finish(0)
+        round_page(nc.vector.tensor_copy, 2 * QCOLS, VECTOR_COLS)
+        finish(1)
+        finish(2)
+        finish(3)
+        for q in range(4):
+            nc.scalar.dma_start(out_2[0, 4 * q : 4 * q + 4, :].bitcast(I32), o_scales[32 * q : 32 * q + 4, :].bitcast(I32))

@@ -20,7 +20,7 @@ P = 128
 PACK = 4
 BLOCKS = 16
 RUN = 8
-VECTOR_COLS = 640
+VECTOR_COLS = 512
 QCOLS = 256
 
 
@@ -33,8 +33,8 @@ def tile_picked_momorderpagez_none_po_kernel(
         banks = ctx.enter_context(tc.psum_pool(name="banks", bufs=7))
         turn = ctx.enter_context(tc.psum_pool(name="turn", bufs=1))
 
-        def sb(name, shape, dtype):
-            return keep.tile(shape, dtype, name=name, align_bytes=64)
+        def sb(name, shape, dtype, tag=None):
+            return keep.tile(shape, dtype, name=name, tag=tag or name, align_bytes=64)
 
         def load_list(name, src):
             t = sb(name, list(src.shape), U16)
@@ -44,14 +44,22 @@ def tile_picked_momorderpagez_none_po_kernel(
         xs = sb("xs", [P, T], U8)
         nc.vector.memset(xs[:].bitcast(I32), 0)
         l_offs = load_list("l_offs", offs)
+        l_two = load_list("l_two", two)
+        wa_raw = [sb("wa_raw%d" % h, [P, PACK, H // 2], F32) for h in range(2)]
+        wa_rows = wa.rearrange("(p j) c -> p j c", j=PACK)
+        nc.sync.dma_start(wa_raw[0][:], wa_rows[:, :, 0:256])
+        for q in range(4):
+            nc.sync.dma_start(xs[32 * q : 32 * q + 4, :].bitcast(I32), x_scales[0, 4 * q : 4 * q + 4, :].bitcast(I32))
+        nc.sync.dma_start(wa_raw[1][:], wa_rows[:, :, 256:512])
         xw = sb("xw", [P, T], I32)
         nc.sync.dma_start(xw[:], x_words[0].rearrange("p c r -> p (c r)").bitcast(I32))
-        for q in range(4):
-            nc.scalar.dma_start(xs[32 * q : 32 * q + 4, :].bitcast(I32), x_scales[0, 4 * q : 4 * q + 4, :].bitcast(I32))
-        wa_raw = [sb("wa_raw%d" % h, [P, PACK, H // 2], F32) for h in range(2)]
-        for h in range(2):
-            nc.sync.dma_start(wa_raw[h][:], wa.rearrange("(p j) c -> p j c", j=PACK)[:, :, h * 256 : (h + 1) * 256])
-        l_two = load_list("l_two", two)
+        rows = sb("rows", [P, P], F32, tag="rows_then_scales")
+        nc.gpsimd.memset(rows[:], 0.0)
+        for i, vec in enumerate((gt, gi)):
+            nc.sync.dma_start(
+                rows[4 * i : 4 * i + 4, :].rearrange("t (b j) -> t b j", j=RUN),
+                vec.rearrange("(b t j) o -> t b (j o)", t=PACK, j=RUN),
+            )
         l_n1 = load_list("l_n1", n1)
         l_n2 = load_list("l_n2", n2)
         wb_raw = sb("wb_raw", [P, PACK, N], F32)
@@ -59,53 +67,47 @@ def tile_picked_momorderpagez_none_po_kernel(
         l_n4 = load_list("l_n4", n4)
         l_n3 = load_list("l_n3", n3)
 
-        rows = sb("rows", [P, P], F32)
-        nc.gpsimd.memset(rows[:], 0.0)
-        for i, vec in enumerate((gt, gi)):
-            nc.gpsimd.dma_start(
-                rows[4 * i : 4 * i + 4, :].rearrange("t (b j) -> t b j", j=RUN),
-                vec.rearrange("(b t j) o -> t b (j o)", t=PACK, j=RUN),
-            )
         ident = sb("ident", [P, P], F32)
         make_identity(nc, ident[:])
-
         pages = [sb("page%d" % t, [P, U], F32) for t in range(PACK)]
         for t in range(PACK):
-            nc.vector.memset(pages[t][:], 0.0)
+            engine = nc.vector if t < 2 else nc.gpsimd
+            engine.memset(pages[t][:].bitcast(I32), 0)
 
         turned = turn.tile([P, P], F32, name="turned")
         nc.tensor.transpose(turned[:], rows[:], ident[:])
-        gt_abs = sb("gt_abs", [P, PACK], F32)
+        gt_abs = sb("gt_abs", [P, PACK], F32, tag="wb_then_ra")
         gt_sign = sb("gt_sign", [P, PACK], F32)
-        gi_sb = sb("gi_sb", [P, PACK], F32)
+        g_sb = sb("g_sb", [P, 2 * PACK], F32)
         gi_signed = sb("gi_signed", [P, PACK], F32)
         nc.scalar.activation(gt_abs[:], turned[:, 0:4], ACT.Abs)
-        nc.scalar.activation(gt_sign[:], turned[:, 0:4], ACT.Sign)
-        nc.scalar.copy(gi_sb[:], turned[:, 4:8])
-        nc.gpsimd.tensor_tensor(gi_signed[:], gi_sb[:], gt_sign[:], ALU.mult)
+        nc.scalar.copy(g_sb[:], turned[:, 0:8])
+        nc.gpsimd.tensor_scalar(gt_sign[:], g_sb[:, 0:4], 0.0, 2.0, ALU.is_ge, ALU.mult)
+        nc.gpsimd.tensor_scalar(gt_sign[:], gt_sign[:], 1.0, -1.0, ALU.mult, ALU.add)
+        nc.gpsimd.tensor_tensor(gi_signed[:], g_sb[:, 4:8], gt_sign[:], ALU.mult)
 
-        def gather_words(name, lst):
-            g = sb(name, [P, S], U32)
+        def gather_words(name, lst, tag=None):
+            g = sb(name, [P, S], U32, tag=tag)
             nc.vector.tensor_copy(
                 g[:].rearrange("p (t b j) -> p b t j", t=PACK, j=RUN), xw[:].bitcast(U32).indirect(lst[:])
             )
             return g
 
-        def gather_bytes(name, lst):
-            g = sb(name, [P, S], U8)
+        def gather_bytes(name, lst, tag=None):
+            g = sb(name, [P, S], U8, tag=tag)
             nc.vector.tensor_copy(g[:], xs[:].indirect(lst[:]))
             return g
 
-        def deal_bytes(name, g):
-            d = sb(name, [P, S], U8)
+        def deal_bytes(name, g, tag=None):
+            d = sb(name, [P, S], U8, tag=tag)
             nc.vector.tensor_copy(
                 d[:].bitcast(I32).rearrange("p (t b w) -> p t b w", t=PACK, w=2),
                 g[:].bitcast(I32).rearrange("p (b t w) -> p t b w", t=PACK, w=2),
             )
             return d
 
-        def round_weights(dst, raw):
-            nc.scalar.copy(
+        def round_weights(engine_copy, dst, raw):
+            engine_copy(
                 dst.rearrange("p (c i t) -> p c t i", i=4, t=PACK), raw.rearrange("p t (c i) -> p c t i", i=4)
             )
 
@@ -121,41 +123,42 @@ def tile_picked_momorderpagez_none_po_kernel(
             )
             return acc
 
-        xa_words = gather_words("xa_words", l_offs)
-        xa_raw = gather_bytes("xa_raw", l_offs)
-        xb_words = gather_words("xb_words", l_two)
-        xa_scales = deal_bytes("xa_scales", xa_raw)
+        xa_raw = gather_bytes("xa_raw", l_offs, tag="bytes_then_words")
+        xb_raw = gather_bytes("xb_raw", l_two)
+        xb_scales = deal_bytes("xb_scales", xb_raw)
 
         wa_bf = sb("wa_bf", [P, H * PACK], BF16)
         wa_codes = sb("wa_codes", [P, H], U32)
         wa_scales = sb("wa_scales", [P, H], U8)
         for h in range(2):
-            round_weights(wa_bf[:, h * 1024 : (h + 1) * 1024], wa_raw[h][:])
+            round_weights(nc.scalar.copy, wa_bf[:, h * 1024 : (h + 1) * 1024], wa_raw[h][:])
         quantize(wa_codes[:], wa_scales[:], wa_bf[:])
 
-        xb_raw = gather_bytes("xb_raw", l_two)
-        xb_scales = deal_bytes("xb_scales", xb_raw)
+        xa_words = gather_words("xa_words", l_offs)
+        xa_scales = deal_bytes("xa_scales", xa_raw, tag="rows_then_scales")
+        xb_words = gather_words("xb_words", l_two, tag="bytes_then_words")
 
         a = [sb("a%d" % t, [P, H], F32) for t in range(PACK)]
         for t in range(PACK):
             acc = product(xa_words, xa_scales, wa_codes, wa_scales, t)
             nc.scalar.activation(a[t][:], acc[:], ACT.Copy, scale=gt_abs[:, t : t + 1])
 
-        wb_bf = sb("wb_bf", [P, N * PACK], BF16)
+        wb_bf = sb("wb_bf", [P, N * PACK], BF16, tag="wb_then_ra")
         wb_codes = sb("wb_codes", [P, N], U32)
         wb_scales = sb("wb_scales", [P, N], U8)
-        round_weights(wb_bf[:], wb_raw[:])
+        round_weights(nc.scalar.copy, wb_bf[:], wb_raw[:])
 
         pa = sb("pa", [P, PACK * W], F32)
         pb = sb("pb", [P, PACK * W], F32)
-        ra = sb("ra", [P, PACK * W], F32)
-        rb = sb("rb", [P, PACK * W], F32)
         for t in range(PACK):
             nc.vector.tensor_copy(pa[:, t * W : (t + 1) * W], a[t][:].indirect(l_n1[:]))
             nc.vector.tensor_copy(pb[:, t * W : (t + 1) * W], a[t][:].indirect(l_n2[:]))
         quantize(wb_codes[:], wb_scales[:], wb_bf[:])
-        nc.vector.tensor_tensor(ra[:], pa[:], pb[:], ALU.max)
-        nc.vector.tensor_tensor(rb[:], pa[:], pb[:], ALU.min)
+        ordered = sb("ordered", [P, 2 * PACK * W], F32, tag="wb_then_ra")
+        ra = ordered[:, 0 : PACK * W]
+        rb = ordered[:, PACK * W : 2 * PACK * W]
+        nc.vector.tensor_tensor(ra, pa[:], pb[:], ALU.max)
+        nc.vector.tensor_tensor(rb, pa[:], pb[:], ALU.min)
 
         z2_bf = sb("z2_bf", [P, N * PACK], BF16)
         z2_view = z2_bf[:].rearrange("p (c t) -> p c t", t=PACK)
@@ -189,8 +192,8 @@ def tile_picked_momorderpagez_none_po_kernel(
             put_larger(t + 1)
             put_smaller(t)
             round_z(t)
-        quantize(z2_codes[:], z2_scales[:], z2_bf[:])
         put_smaller(3)
+        quantize(z2_codes[:], z2_scales[:], z2_bf[:])
 
         last = dt[3][:].rearrange("p (m u) -> p m u", u=PACK)
 
@@ -209,10 +212,12 @@ def tile_picked_momorderpagez_none_po_kernel(
         cv = [sb("cv%d" % u, [P, N], F32) for u in range(PACK)]
         pos = [sb("pos%d" % u, [P, N], F32) for u in range(PACK)]
         neg = [sb("neg%d" % u, [P, N], F32) for u in range(PACK)]
+        accs = [product(z_codes, z_scales, z2_codes, z2_scales, u) for u in range(PACK)]
+        nc.scalar.activation(pos[0][:], accs[0][:], ACT.Relu, scale=0.0625)
         for u in range(PACK):
-            acc = product(z_codes, z_scales, z2_codes, z2_scales, u)
-            nc.scalar.activation(pos[u][:], acc[:], ACT.Relu, scale=0.0625)
-            nc.scalar.activation(cv[u][:], acc[:], ACT.Copy, scale=0.0625)
+            if u + 1 < PACK:
+                nc.scalar.activation(pos[u + 1][:], accs[u + 1][:], ACT.Relu, scale=0.0625)
+            nc.scalar.activation(cv[u][:], accs[u][:], ACT.Copy, scale=0.0625)
 
         page_bf = sb("page_bf", [P, U * PACK], BF16)
         page_view = page_bf[:].rearrange("p (c t) -> p c t", t=PACK)
@@ -256,7 +261,6 @@ def tile_picked_momorderpagez_none_po_kernel(
         round_page(nc.vector.tensor_copy, 0, QCOLS)
         round_page(nc.vector.tensor_copy, QCOLS, 2 * QCOLS)
         finish(0)
-        round_page(nc.vector.tensor_copy, 2 * QCOLS, VECTOR_COLS)
         finish(1)
         finish(2)
         finish(3)

@@ -45,12 +45,11 @@ def tile_picked_momorderpagez_none_po_kernel(
         nc.vector.memset(xs[:].bitcast(I32), 0)
         l_offs = load_list("l_offs", offs)
         l_two = load_list("l_two", two)
-        wa_raw = [sb("wa_raw%d" % h, [P, PACK, H // 2], F32) for h in range(2)]
+        wa_raw = [sb("wa_raw%d" % h, [P, PACK, W], F32) for h in range(2)]
         wa_rows = wa.rearrange("(p j) c -> p j c", j=PACK)
         nc.sync.dma_start(wa_raw[0][:], wa_rows[:, :, 0:256])
         for q in range(4):
             nc.sync.dma_start(xs[32 * q : 32 * q + 4, :].bitcast(I32), x_scales[0, 4 * q : 4 * q + 4, :].bitcast(I32))
-        nc.sync.dma_start(wa_raw[1][:], wa_rows[:, :, 256:512])
         xw = sb("xw", [P, T], I32)
         nc.sync.dma_start(xw[:], x_words[0].rearrange("p c r -> p (c r)").bitcast(I32))
         rows = sb("rows", [P, P], F32, tag="rows_then_scales")
@@ -60,6 +59,7 @@ def tile_picked_momorderpagez_none_po_kernel(
                 rows[4 * i : 4 * i + 4, :].rearrange("t (b j) -> t b j", j=RUN),
                 vec.rearrange("(b t j) o -> t b (j o)", t=PACK, j=RUN),
             )
+        nc.sync.dma_start(wa_raw[1][:], wa_rows[:, :, 256:512])
         l_n1 = load_list("l_n1", n1)
         l_n2 = load_list("l_n2", n2)
         wb_raw = sb("wb_raw", [P, PACK, N], F32)
@@ -76,11 +76,9 @@ def tile_picked_momorderpagez_none_po_kernel(
 
         turned = turn.tile([P, P], F32, name="turned")
         nc.tensor.transpose(turned[:], rows[:], ident[:])
-        gt_abs = sb("gt_abs", [P, PACK], F32, tag="wb_then_ra")
         gt_sign = sb("gt_sign", [P, PACK], F32)
         g_sb = sb("g_sb", [P, 2 * PACK], F32)
         gi_signed = sb("gi_signed", [P, PACK], F32)
-        nc.scalar.activation(gt_abs[:], turned[:, 0:4], ACT.Abs)
         nc.scalar.copy(g_sb[:], turned[:, 0:8])
         nc.gpsimd.tensor_scalar(gt_sign[:], g_sb[:, 0:4], 0.0, 2.0, ALU.is_ge, ALU.mult)
         nc.gpsimd.tensor_scalar(gt_sign[:], gt_sign[:], 1.0, -1.0, ALU.mult, ALU.add)
@@ -114,34 +112,43 @@ def tile_picked_momorderpagez_none_po_kernel(
         def quantize(codes, scales, src):
             nc.vector.quantize_mx(out=codes.bitcast(FP8X4), scales=scales, in_=src)
 
-        def product(lc, ls, rc, rs, t):
-            acc = banks.tile([P, 512], F32, name="acc")
+        def product(lc, ls, rc, rs, t, moving=slice(0, 512)):
+            bank = banks.tile([P, 512], F32, name="bank")
+            acc = bank[:, 0 : moving.stop - moving.start]
             cols = slice(t * P, (t + 1) * P)
             nc.tensor.matmul_mx(
-                out=acc[:], lhsT=lc[:, cols].bitcast(FP8X4), lhsT_scale=ls[:, cols],
-                rhs=rc[:].bitcast(FP8X4), rhs_scale=rs[:], start=True, stop=True,
+                out=acc, lhsT=lc[:, cols].bitcast(FP8X4), lhsT_scale=ls[:, cols],
+                rhs=rc[:, moving].bitcast(FP8X4), rhs_scale=rs[:, moving], start=True, stop=True,
             )
             return acc
 
-        xa_raw = gather_bytes("xa_raw", l_offs, tag="bytes_then_words")
+        xa_raw = gather_bytes("xa_raw", l_offs)
         xb_raw = gather_bytes("xb_raw", l_two)
         xb_scales = deal_bytes("xb_scales", xb_raw)
 
-        wa_bf = sb("wa_bf", [P, H * PACK], BF16)
+        gt_abs = sb("gt_abs", [P, PACK], F32, tag="wb_then_ra")
+        nc.scalar.activation(gt_abs[:], turned[:, 0:4], ACT.Abs)
+
+        wa_bf = [sb("wa_bf0", [P, W * PACK], BF16), sb("wa_bf1", [P, W * PACK], BF16, tag="wa_then_words")]
         wa_codes = sb("wa_codes", [P, H], U32)
         wa_scales = sb("wa_scales", [P, H], U8)
-        for h in range(2):
-            round_weights(nc.scalar.copy, wa_bf[:, h * 1024 : (h + 1) * 1024], wa_raw[h][:])
-        quantize(wa_codes[:], wa_scales[:], wa_bf[:])
+        halves = [slice(h * W, (h + 1) * W) for h in range(2)]
 
+        def prepare_wa(h, engine_copy):
+            round_weights(engine_copy, wa_bf[h][:], wa_raw[h][:])
+            quantize(wa_codes[:, halves[h]], wa_scales[:, halves[h]], wa_bf[h][:])
+
+        prepare_wa(0, nc.scalar.copy)
         xa_words = gather_words("xa_words", l_offs)
         xa_scales = deal_bytes("xa_scales", xa_raw, tag="rows_then_scales")
-        xb_words = gather_words("xb_words", l_two, tag="bytes_then_words")
+        prepare_wa(1, nc.vector.tensor_copy)
+        xb_words = gather_words("xb_words", l_two, tag="wa_then_words")
 
         a = [sb("a%d" % t, [P, H], F32) for t in range(PACK)]
         for t in range(PACK):
-            acc = product(xa_words, xa_scales, wa_codes, wa_scales, t)
-            nc.scalar.activation(a[t][:], acc[:], ACT.Copy, scale=gt_abs[:, t : t + 1])
+            for cols in halves:
+                acc = product(xa_words, xa_scales, wa_codes, wa_scales, t, cols)
+                nc.scalar.activation(a[t][:, cols], acc, ACT.Copy, scale=gt_abs[:, t : t + 1])
 
         wb_bf = sb("wb_bf", [P, N * PACK], BF16, tag="wb_then_ra")
         wb_codes = sb("wb_codes", [P, N], U32)
@@ -160,13 +167,16 @@ def tile_picked_momorderpagez_none_po_kernel(
         nc.vector.tensor_tensor(ra, pa[:], pb[:], ALU.max)
         nc.vector.tensor_tensor(rb, pa[:], pb[:], ALU.min)
 
-        z2_bf = sb("z2_bf", [P, N * PACK], BF16)
-        z2_view = z2_bf[:].rearrange("p (c t) -> p c t", t=PACK)
+        z2_bf = [sb("z2_bf%d" % h, [P, W * PACK], BF16, tag="z2_then_dt%d" % h) for h in range(2)]
         for t in range(PACK):
             acc = product(xb_words, xb_scales, wb_codes, wb_scales, t)
-            nc.scalar.activation(z2_view[:, :, t], acc[:], ACT.Copy, scale=gi_signed[:, t : t + 1])
+            for h in range(2):
+                nc.scalar.activation(
+                    z2_bf[h][:].rearrange("p (c t) -> p c t", t=PACK)[:, :, t],
+                    acc[:, h * W : (h + 1) * W], ACT.Copy, scale=gi_signed[:, t : t + 1],
+                )
 
-        dt = [sb("dt%d" % t, [P, H], F32) for t in range(PACK)]
+        dt = {t: sb("dt%d" % t, [P, H], F32) for t in (2, 0)}
         z_bf = sb("z_bf", [P, H * PACK], BF16)
         z_view = z_bf[:].rearrange("p (u m t) -> p m u t", u=PACK, t=PACK)
         z_codes = sb("z_codes", [P, H], U32)
@@ -187,13 +197,20 @@ def tile_picked_momorderpagez_none_po_kernel(
             else:
                 nc.scalar.copy(z_view[:, :, :, t], src)
 
-        put_larger(0)
-        for t in range(PACK - 1):
-            put_larger(t + 1)
+        for t in (2, 0):
+            put_larger(t)
+        for t in (2, 0):
             put_smaller(t)
             round_z(t)
+        for h, t in enumerate((1, 3)):
+            cols = slice(h * W, (h + 1) * W)
+            quantize(z2_codes[:, cols], z2_scales[:, cols], z2_bf[h][:])
+            dt[t] = sb("dt%d" % t, [P, H], F32, tag="z2_then_dt%d" % h)
+        for t in (1, 3):
+            put_larger(t)
+        put_smaller(1)
+        round_z(1)
         put_smaller(3)
-        quantize(z2_codes[:], z2_scales[:], z2_bf[:])
 
         last = dt[3][:].rearrange("p (m u) -> p m u", u=PACK)
 
@@ -203,21 +220,28 @@ def tile_picked_momorderpagez_none_po_kernel(
         def quantize_z(u):
             quantize(z_codes[:, u * P : (u + 1) * P], z_scales[:, u * P : (u + 1) * P], z_bf[:, u * 512 : (u + 1) * 512])
 
-        round_last(0)
-        for u in range(PACK):
-            if u + 1 < PACK:
-                round_last(u + 1)
+        order = (2, 0, 1, 3)
+        round_last(order[0])
+        for i, u in enumerate(order):
+            if i + 1 < PACK:
+                round_last(order[i + 1])
             quantize_z(u)
 
         cv = [sb("cv%d" % u, [P, N], F32) for u in range(PACK)]
         pos = [sb("pos%d" % u, [P, N], F32) for u in range(PACK)]
         neg = [sb("neg%d" % u, [P, N], F32) for u in range(PACK)]
-        accs = [product(z_codes, z_scales, z2_codes, z2_scales, u) for u in range(PACK)]
-        nc.scalar.activation(pos[0][:], accs[0][:], ACT.Relu, scale=0.0625)
-        for u in range(PACK):
-            if u + 1 < PACK:
-                nc.scalar.activation(pos[u + 1][:], accs[u + 1][:], ACT.Relu, scale=0.0625)
-            nc.scalar.activation(cv[u][:], accs[u][:], ACT.Copy, scale=0.0625)
+        pieces = {u: halves if u == order[0] else [slice(0, N)] for u in order}
+        accs = {u: [product(z_codes, z_scales, z2_codes, z2_scales, u, cols) for cols in pieces[u]] for u in order}
+
+        def empty(dst, u, func):
+            for cols, acc in zip(pieces[u], accs[u]):
+                nc.scalar.activation(dst[u][:, cols], acc, func, scale=0.0625)
+
+        empty(pos, order[0], ACT.Relu)
+        for i, u in enumerate(order):
+            if i + 1 < PACK:
+                empty(pos, order[i + 1], ACT.Relu)
+            empty(cv, u, ACT.Copy)
 
         page_bf = sb("page_bf", [P, U * PACK], BF16)
         page_view = page_bf[:].rearrange("p (c t) -> p c t", t=PACK)
@@ -234,9 +258,9 @@ def tile_picked_momorderpagez_none_po_kernel(
             nc.vector.tensor_tensor(pages[u][:].indirect(l_n3[:]), cv[u][:], neg[u][:], ALU.add)
             nc.sync.dma_start(out_rows[:, u, :], pages[u][:])
 
-        fetch(0)
-        for u in range(PACK - 1):
-            fetch(u + 1)
+        fetch(order[0])
+        for i, u in enumerate(order[:-1]):
+            fetch(order[i + 1])
             put_page(u)
             if u == 2:
                 nc.scalar.copy(page_view[:, :, 2:4], pages[u][:].unsqueeze(2).to_broadcast([P, U, 2]))
@@ -254,7 +278,9 @@ def tile_picked_momorderpagez_none_po_kernel(
         def finish(i):
             cols = slice(i * QCOLS, (i + 1) * QCOLS)
             quantize(o_codes[:, cols], o_scales[:, cols], page_bf[:, i * QCOLS * PACK : (i + 1) * QCOLS * PACK])
-            nc.sync.dma_start(words_out[:, cols], o_codes[:, cols].bitcast(I32))
+            if i > 0:
+                done = slice(0 if i == 1 else cols.start, cols.stop)
+                nc.sync.dma_start(words_out[:, done], o_codes[:, done].bitcast(I32))
 
         round_page(nc.scalar.copy, VECTOR_COLS, 3 * QCOLS)
         round_page(nc.scalar.copy, 3 * QCOLS, U)

@@ -17,11 +17,16 @@ ALU = mybir.AluOpType
 ACT = mybir.ActivationFunctionType
 
 P = 128
-PACK = 4
-BLOCKS = 16
+PLANES = 4
 RUN = 8
-VECTOR_COLS = 512
-QCOLS = 256
+QUADRANT = 32
+SCALE_ROWS = 4
+LINE = 4
+HALVES = [slice(0, W), slice(W, 2 * W)]
+QUARTER = U // 4
+CV_SCALE = 0.0625
+ORDER = (2, 0, 1, 3)
+FIRST, LAST = ORDER[0], ORDER[-1]
 
 
 def tile_picked_momorderpagez_none_po_kernel(
@@ -37,258 +42,245 @@ def tile_picked_momorderpagez_none_po_kernel(
             return keep.tile(shape, dtype, name=name, tag=tag or name, align_bytes=64)
 
         def load_list(name, src):
-            t = sb(name, list(src.shape), U16)
-            nc.sync.dma_start(t[:], src)
-            return t
+            tile = sb(name, list(src.shape), U16)
+            nc.sync.dma_start(tile[:], src)
+            return tile
 
         xs = sb("xs", [P, T], U8)
         nc.vector.memset(xs[:].bitcast(I32), 0)
         l_offs = load_list("l_offs", offs)
         l_two = load_list("l_two", two)
-        wa_raw = [sb("wa_raw%d" % h, [P, PACK, W], F32) for h in range(2)]
-        wa_rows = wa.rearrange("(p j) c -> p j c", j=PACK)
-        nc.sync.dma_start(wa_raw[0][:], wa_rows[:, :, 0:256])
-        for q in range(4):
-            nc.sync.dma_start(xs[32 * q : 32 * q + 4, :].bitcast(I32), x_scales[0, 4 * q : 4 * q + 4, :].bitcast(I32))
+        wa_raw = [sb("wa_raw%d" % h, [P, PLANES, W], F32) for h in range(2)]
+        wa_rows = wa.rearrange("(p j) c -> p j c", j=PLANES)
+        nc.sync.dma_start(wa_raw[0][:], wa_rows[:, :, HALVES[0]])
+        for r in range(SCALE_ROWS):
+            nc.sync.dma_start(xs[r:P:QUADRANT, :].bitcast(I32), x_scales[0, r::SCALE_ROWS, :].bitcast(I32))
         xw = sb("xw", [P, T], I32)
         nc.sync.dma_start(xw[:], x_words[0].rearrange("p c r -> p (c r)").bitcast(I32))
-        rows = sb("rows", [P, P], F32, tag="rows_then_scales")
-        nc.gpsimd.memset(rows[:], 0.0)
+        g_rows = sb("g_rows", [P, P], F32, tag="g_rows_then_scales")
+        nc.gpsimd.memset(g_rows[:], 0.0)
         for i, vec in enumerate((gt, gi)):
             nc.sync.dma_start(
-                rows[4 * i : 4 * i + 4, :].rearrange("t (b j) -> t b j", j=RUN),
-                vec.rearrange("(b t j) o -> t b (j o)", t=PACK, j=RUN),
+                g_rows[PLANES * i : PLANES * (i + 1), :].rearrange("t (b j) -> t b j", j=RUN),
+                vec.rearrange("(b t j) o -> t b (j o)", t=PLANES, j=RUN),
             )
-        nc.sync.dma_start(wa_raw[1][:], wa_rows[:, :, 256:512])
+        nc.sync.dma_start(wa_raw[1][:], wa_rows[:, :, HALVES[1]])
         l_n1 = load_list("l_n1", n1)
         l_n2 = load_list("l_n2", n2)
-        wb_raw = sb("wb_raw", [P, PACK, N], F32)
-        nc.sync.dma_start(wb_raw[:], wb.rearrange("(p j) c -> p j c", j=PACK))
+        wb_raw = sb("wb_raw", [P, PLANES, N], F32)
+        nc.sync.dma_start(wb_raw[:], wb.rearrange("(p j) c -> p j c", j=PLANES))
         l_n4 = load_list("l_n4", n4)
         l_n3 = load_list("l_n3", n3)
 
         ident = sb("ident", [P, P], F32)
         make_identity(nc, ident[:])
-        pages = [sb("page%d" % t, [P, U], F32) for t in range(PACK)]
-        for t in range(PACK):
-            engine = nc.vector if t < 2 else nc.gpsimd
+        pages = [sb("page%d" % t, [P, U], F32) for t in range(PLANES)]
+        for t in range(PLANES):
+            engine = nc.vector if t < PLANES // 2 else nc.gpsimd
             engine.memset(pages[t][:].bitcast(I32), 0)
 
         turned = turn.tile([P, P], F32, name="turned")
-        nc.tensor.transpose(turned[:], rows[:], ident[:])
-        gt_sign = sb("gt_sign", [P, PACK], F32)
-        g_sb = sb("g_sb", [P, 2 * PACK], F32)
-        gi_signed = sb("gi_signed", [P, PACK], F32)
-        nc.scalar.copy(g_sb[:], turned[:, 0:8])
-        nc.gpsimd.tensor_scalar(gt_sign[:], g_sb[:, 0:4], 0.0, 2.0, ALU.is_ge, ALU.mult)
+        nc.tensor.transpose(turned[:], g_rows[:], ident[:])
+        gt_sign = sb("gt_sign", [P, PLANES], F32)
+        g_cols = sb("g_cols", [P, 2 * PLANES], F32)
+        gi_signed = sb("gi_signed", [P, PLANES], F32)
+        nc.scalar.copy(g_cols[:], turned[:, 0 : 2 * PLANES])
+        nc.gpsimd.tensor_scalar(gt_sign[:], g_cols[:, 0:PLANES], 0.0, 2.0, ALU.is_ge, ALU.mult)
         nc.gpsimd.tensor_scalar(gt_sign[:], gt_sign[:], 1.0, -1.0, ALU.mult, ALU.add)
-        nc.gpsimd.tensor_tensor(gi_signed[:], g_sb[:, 4:8], gt_sign[:], ALU.mult)
+        nc.gpsimd.tensor_tensor(gi_signed[:], g_cols[:, PLANES : 2 * PLANES], gt_sign[:], ALU.mult)
 
         def gather_words(name, lst, tag=None):
-            g = sb(name, [P, S], U32, tag=tag)
+            words = sb(name, [P, S], U32, tag=tag)
             nc.vector.tensor_copy(
-                g[:].rearrange("p (t b j) -> p b t j", t=PACK, j=RUN), xw[:].bitcast(U32).indirect(lst[:])
+                words[:].rearrange("p (t b j) -> p b t j", t=PLANES, j=RUN), xw[:].bitcast(U32).indirect(lst[:])
             )
-            return g
+            return words
 
-        def gather_bytes(name, lst, tag=None):
-            g = sb(name, [P, S], U8, tag=tag)
-            nc.vector.tensor_copy(g[:], xs[:].indirect(lst[:]))
-            return g
+        def gather_bytes(name, lst):
+            picked = sb(name, [P, S], U8)
+            nc.vector.tensor_copy(picked[:], xs[:].indirect(lst[:]))
+            return picked
 
-        def deal_bytes(name, g, tag=None):
-            d = sb(name, [P, S], U8, tag=tag)
+        def deal_bytes(name, picked, tag=None):
+            dealt = sb(name, [P, S], U8, tag=tag)
             nc.vector.tensor_copy(
-                d[:].bitcast(I32).rearrange("p (t b w) -> p t b w", t=PACK, w=2),
-                g[:].bitcast(I32).rearrange("p (b t w) -> p t b w", t=PACK, w=2),
+                dealt[:].bitcast(I32).rearrange("p (t b w) -> p t b w", t=PLANES, w=2),
+                picked[:].bitcast(I32).rearrange("p (b t w) -> p t b w", t=PLANES, w=2),
             )
-            return d
+            return dealt
 
         def round_weights(engine_copy, dst, raw):
             engine_copy(
-                dst.rearrange("p (c i t) -> p c t i", i=4, t=PACK), raw.rearrange("p t (c i) -> p c t i", i=4)
+                dst.rearrange("p (c i t) -> p c t i", i=LINE, t=PLANES), raw.rearrange("p t (c i) -> p c t i", i=LINE)
             )
 
         def quantize(codes, scales, src):
             nc.vector.quantize_mx(out=codes.bitcast(FP8X4), scales=scales, in_=src)
 
-        def product(lc, ls, rc, rs, t, moving=slice(0, 512)):
-            bank = banks.tile([P, 512], F32, name="bank")
+        def product(left_codes, left_scales, right_codes, right_scales, t, moving=slice(0, N)):
+            bank = banks.tile([P, N], F32, name="bank")
             acc = bank[:, 0 : moving.stop - moving.start]
-            cols = slice(t * P, (t + 1) * P)
+            fixed = slice(t * P, (t + 1) * P)
             nc.tensor.matmul_mx(
-                out=acc, lhsT=lc[:, cols].bitcast(FP8X4), lhsT_scale=ls[:, cols],
-                rhs=rc[:, moving].bitcast(FP8X4), rhs_scale=rs[:, moving], start=True, stop=True,
+                out=acc, lhsT=left_codes[:, fixed].bitcast(FP8X4), lhsT_scale=left_scales[:, fixed],
+                rhs=right_codes[:, moving].bitcast(FP8X4), rhs_scale=right_scales[:, moving], start=True, stop=True,
             )
             return acc
 
-        xa_raw = gather_bytes("xa_raw", l_offs)
-        xb_raw = gather_bytes("xb_raw", l_two)
-        xb_scales = deal_bytes("xb_scales", xb_raw)
+        xa_picked = gather_bytes("xa_picked", l_offs)
+        xb_picked = gather_bytes("xb_picked", l_two)
+        xb_scales = deal_bytes("xb_scales", xb_picked)
 
-        gt_abs = sb("gt_abs", [P, PACK], F32, tag="wb_then_ra")
-        nc.scalar.activation(gt_abs[:], turned[:, 0:4], ACT.Abs)
+        gt_abs = sb("gt_abs", [P, PLANES], F32, tag="gt_wb_pairs")
+        nc.scalar.activation(gt_abs[:], turned[:, 0:PLANES], ACT.Abs)
 
-        wa_bf = [sb("wa_bf0", [P, W * PACK], BF16), sb("wa_bf1", [P, W * PACK], BF16, tag="wa_then_words")]
+        wa_bf = [sb("wa_bf0", [P, W * PLANES], BF16), sb("wa_bf1", [P, W * PLANES], BF16, tag="wa_then_words")]
         wa_codes = sb("wa_codes", [P, H], U32)
         wa_scales = sb("wa_scales", [P, H], U8)
-        halves = [slice(h * W, (h + 1) * W) for h in range(2)]
 
         def prepare_wa(h, engine_copy):
             round_weights(engine_copy, wa_bf[h][:], wa_raw[h][:])
-            quantize(wa_codes[:, halves[h]], wa_scales[:, halves[h]], wa_bf[h][:])
+            quantize(wa_codes[:, HALVES[h]], wa_scales[:, HALVES[h]], wa_bf[h][:])
 
         prepare_wa(0, nc.scalar.copy)
         xa_words = gather_words("xa_words", l_offs)
-        xa_scales = deal_bytes("xa_scales", xa_raw, tag="rows_then_scales")
+        xa_scales = deal_bytes("xa_scales", xa_picked, tag="g_rows_then_scales")
         prepare_wa(1, nc.vector.tensor_copy)
         xb_words = gather_words("xb_words", l_two, tag="wa_then_words")
 
-        a = [sb("a%d" % t, [P, H], F32) for t in range(PACK)]
-        for t in range(PACK):
-            for cols in halves:
+        a = [sb("a%d" % t, [P, H], F32) for t in range(PLANES)]
+        for t in range(PLANES):
+            for cols in HALVES:
                 acc = product(xa_words, xa_scales, wa_codes, wa_scales, t, cols)
                 nc.scalar.activation(a[t][:, cols], acc, ACT.Copy, scale=gt_abs[:, t : t + 1])
 
-        wb_bf = sb("wb_bf", [P, N * PACK], BF16, tag="wb_then_ra")
+        wb_bf = sb("wb_bf", [P, N * PLANES], BF16, tag="gt_wb_pairs")
         wb_codes = sb("wb_codes", [P, N], U32)
         wb_scales = sb("wb_scales", [P, N], U8)
         round_weights(nc.scalar.copy, wb_bf[:], wb_raw[:])
 
-        pa = sb("pa", [P, PACK * W], F32)
-        pb = sb("pb", [P, PACK * W], F32)
-        for t in range(PACK):
+        pa = sb("pa", [P, PLANES * W], F32)
+        pb = sb("pb", [P, PLANES * W], F32)
+        for t in range(PLANES):
             nc.vector.tensor_copy(pa[:, t * W : (t + 1) * W], a[t][:].indirect(l_n1[:]))
             nc.vector.tensor_copy(pb[:, t * W : (t + 1) * W], a[t][:].indirect(l_n2[:]))
         quantize(wb_codes[:], wb_scales[:], wb_bf[:])
-        ordered = sb("ordered", [P, 2 * PACK * W], F32, tag="wb_then_ra")
-        ra = ordered[:, 0 : PACK * W]
-        rb = ordered[:, PACK * W : 2 * PACK * W]
+        pairs = sb("pairs", [P, 2 * PLANES * W], F32, tag="gt_wb_pairs")
+        ra = pairs[:, 0 : PLANES * W]
+        rb = pairs[:, PLANES * W : 2 * PLANES * W]
         nc.vector.tensor_tensor(ra, pa[:], pb[:], ALU.max)
         nc.vector.tensor_tensor(rb, pa[:], pb[:], ALU.min)
 
-        z2_bf = [sb("z2_bf%d" % h, [P, W * PACK], BF16, tag="z2_then_dt%d" % h) for h in range(2)]
-        for t in range(PACK):
+        z2_bf = [sb("z2_bf%d" % h, [P, W * PLANES], BF16, tag="z2_then_z%d" % h) for h in range(2)]
+        for t in range(PLANES):
             acc = product(xb_words, xb_scales, wb_codes, wb_scales, t)
             for h in range(2):
                 nc.scalar.activation(
-                    z2_bf[h][:].rearrange("p (c t) -> p c t", t=PACK)[:, :, t],
-                    acc[:, h * W : (h + 1) * W], ACT.Copy, scale=gi_signed[:, t : t + 1],
+                    z2_bf[h][:].rearrange("p (c t) -> p c t", t=PLANES)[:, :, t],
+                    acc[:, HALVES[h]], ACT.Copy, scale=gi_signed[:, t : t + 1],
                 )
 
-        dt = {t: sb("dt%d" % t, [P, H], F32) for t in (2, 0)}
-        z_bf = sb("z_bf", [P, H * PACK], BF16)
-        z_view = z_bf[:].rearrange("p (u m t) -> p m u t", u=PACK, t=PACK)
+        early, late = ORDER[:2], ORDER[2:]
+        z = {t: sb("z%d" % t, [P, H], F32) for t in early}
+        z_bf = sb("z_bf", [P, H * PLANES], BF16)
+        z_view = z_bf[:].rearrange("p (u m t) -> p m u t", u=PLANES, t=PLANES)
         z_codes = sb("z_codes", [P, H], U32)
         z_scales = sb("z_scales", [P, H], U8)
         z2_codes = sb("z2_codes", [P, N], U32)
         z2_scales = sb("z2_scales", [P, N], U8)
 
         def put_larger(t):
-            nc.vector.tensor_copy(dt[t][:].indirect(l_n1[:]), ra[:, t * W : (t + 1) * W])
+            nc.vector.tensor_copy(z[t][:].indirect(l_n1[:]), ra[:, t * W : (t + 1) * W])
 
         def put_smaller(t):
-            nc.vector.tensor_copy(dt[t][:].indirect(l_n2[:]), rb[:, t * W : (t + 1) * W])
+            nc.vector.tensor_copy(z[t][:].indirect(l_n2[:]), rb[:, t * W : (t + 1) * W])
 
-        def round_z(t):
-            src = dt[t][:].rearrange("p (m u) -> p m u", u=PACK)
-            if t == 2:
-                nc.scalar.copy(z_view[:, :, :, 2:4], src.unsqueeze(3).to_broadcast([P, P, PACK, 2]))
+        def round_plane(view, t, src):
+            lead = tuple(slice(None) for axis in src.shape)
+            if t == FIRST:
+                nc.scalar.copy(view[lead + (slice(FIRST, LAST + 1),)], src.unsqueeze(src.ndim).to_broadcast(list(src.shape) + [2]))
             else:
-                nc.scalar.copy(z_view[:, :, :, t], src)
+                nc.scalar.copy(view[lead + (t,)], src)
 
-        for t in (2, 0):
+        def z_columns(t):
+            return z[t][:].rearrange("p (m u) -> p m u", u=PLANES)
+
+        for t in early:
             put_larger(t)
-        for t in (2, 0):
+        for t in early:
             put_smaller(t)
-            round_z(t)
-        for h, t in enumerate((1, 3)):
-            cols = slice(h * W, (h + 1) * W)
-            quantize(z2_codes[:, cols], z2_scales[:, cols], z2_bf[h][:])
-            dt[t] = sb("dt%d" % t, [P, H], F32, tag="z2_then_dt%d" % h)
-        for t in (1, 3):
+            round_plane(z_view, t, z_columns(t))
+        for h, t in enumerate(late):
+            quantize(z2_codes[:, HALVES[h]], z2_scales[:, HALVES[h]], z2_bf[h][:])
+            z[t] = sb("z%d" % t, [P, H], F32, tag="z2_then_z%d" % h)
+        for t in late:
             put_larger(t)
-        put_smaller(1)
-        round_z(1)
-        put_smaller(3)
+        put_smaller(late[0])
+        round_plane(z_view, late[0], z_columns(late[0]))
+        put_smaller(LAST)
 
-        last = dt[3][:].rearrange("p (m u) -> p m u", u=PACK)
-
-        def round_last(u):
-            nc.vector.tensor_copy(z_view[:, :, u, 3], last[:, :, u])
+        def round_last_z(u):
+            nc.vector.tensor_copy(z_view[:, :, u, LAST], z_columns(LAST)[:, :, u])
 
         def quantize_z(u):
-            quantize(z_codes[:, u * P : (u + 1) * P], z_scales[:, u * P : (u + 1) * P], z_bf[:, u * 512 : (u + 1) * 512])
+            words = slice(u * P, (u + 1) * P)
+            quantize(z_codes[:, words], z_scales[:, words], z_bf[:, u * P * PLANES : (u + 1) * P * PLANES])
 
-        order = (2, 0, 1, 3)
-        round_last(order[0])
-        for i, u in enumerate(order):
-            if i + 1 < PACK:
-                round_last(order[i + 1])
+        round_last_z(FIRST)
+        for i, u in enumerate(ORDER):
+            if u != LAST:
+                round_last_z(ORDER[i + 1])
             quantize_z(u)
 
-        cv = [sb("cv%d" % u, [P, N], F32) for u in range(PACK)]
-        pos = [sb("pos%d" % u, [P, N], F32) for u in range(PACK)]
-        neg = [sb("neg%d" % u, [P, N], F32) for u in range(PACK)]
-        pieces = {u: halves if u == order[0] else [slice(0, N)] for u in order}
-        accs = {u: [product(z_codes, z_scales, z2_codes, z2_scales, u, cols) for cols in pieces[u]] for u in order}
+        cv = [sb("cv%d" % u, [P, N], F32) for u in range(PLANES)]
+        pos = [sb("pos%d" % u, [P, N], F32) for u in range(PLANES)]
+        neg = [sb("neg%d" % u, [P, N], F32) for u in range(PLANES)]
+        pieces = {u: HALVES if u == FIRST else [slice(0, N)] for u in ORDER}
+        accs = {u: [product(z_codes, z_scales, z2_codes, z2_scales, u, cols) for cols in pieces[u]] for u in ORDER}
 
         def empty(dst, u, func):
             for cols, acc in zip(pieces[u], accs[u]):
-                nc.scalar.activation(dst[u][:, cols], acc, func, scale=0.0625)
+                nc.scalar.activation(dst[u][:, cols], acc, func, scale=CV_SCALE)
 
-        empty(pos, order[0], ACT.Relu)
-        for i, u in enumerate(order):
-            if i + 1 < PACK:
-                empty(pos, order[i + 1], ACT.Relu)
+        empty(pos, FIRST, ACT.Relu)
+        for i, u in enumerate(ORDER):
+            if u != LAST:
+                empty(pos, ORDER[i + 1], ACT.Relu)
             empty(cv, u, ACT.Copy)
 
-        page_bf = sb("page_bf", [P, U * PACK], BF16)
-        page_view = page_bf[:].rearrange("p (c t) -> p c t", t=PACK)
-        out_rows = out_0.rearrange("(p t) c -> p t c", t=PACK)
+        page_bf = sb("page_bf", [P, U * PLANES], BF16)
+        page_view = page_bf[:].rearrange("p (c t) -> p c t", t=PLANES)
+        out_rows = out_0.rearrange("(p t) c -> p t c", t=PLANES)
 
         def fetch(u):
             for h in range(2):
-                nc.vector.tensor_scalar(
-                    neg[u][:, h * W : (h + 1) * W], pos[u][:].indirect(l_n4[:, h * 16 : (h + 1) * 16]),
-                    -1.0, 0.0, ALU.mult, ALU.add,
-                )
+                entries = l_n4[:, h * (W // 16) : (h + 1) * (W // 16)]
+                nc.vector.tensor_scalar(neg[u][:, HALVES[h]], pos[u][:].indirect(entries), -1.0, 0.0, ALU.mult, ALU.add)
 
         def put_page(u):
             nc.vector.tensor_tensor(pages[u][:].indirect(l_n3[:]), cv[u][:], neg[u][:], ALU.add)
             nc.sync.dma_start(out_rows[:, u, :], pages[u][:])
 
-        fetch(order[0])
-        for i, u in enumerate(order[:-1]):
-            fetch(order[i + 1])
+        fetch(FIRST)
+        for i, u in enumerate(ORDER[:-1]):
+            fetch(ORDER[i + 1])
             put_page(u)
-            if u == 2:
-                nc.scalar.copy(page_view[:, :, 2:4], pages[u][:].unsqueeze(2).to_broadcast([P, U, 2]))
-            else:
-                nc.scalar.copy(page_view[:, :, u], pages[u][:])
-        put_page(3)
+            round_plane(page_view, u, pages[u][:])
+        put_page(LAST)
 
         o_codes = sb("o_codes", [P, U], U32)
         o_scales = sb("o_scales", [P, U], U8)
         words_out = out_1[0].rearrange("p c r -> p (c r)").bitcast(I32)
+        quarters = [slice(i * QUARTER, (i + 1) * QUARTER) for i in range(4)]
 
-        def round_page(engine_copy, c0, c1):
-            engine_copy(page_view[:, c0:c1, 3], pages[3][:, c0:c1])
-
-        def finish(i):
-            cols = slice(i * QCOLS, (i + 1) * QCOLS)
-            quantize(o_codes[:, cols], o_scales[:, cols], page_bf[:, i * QCOLS * PACK : (i + 1) * QCOLS * PACK])
-            if i > 0:
-                done = slice(0 if i == 1 else cols.start, cols.stop)
-                nc.sync.dma_start(words_out[:, done], o_codes[:, done].bitcast(I32))
-
-        round_page(nc.scalar.copy, VECTOR_COLS, 3 * QCOLS)
-        round_page(nc.scalar.copy, 3 * QCOLS, U)
-        round_page(nc.vector.tensor_copy, 0, QCOLS)
-        round_page(nc.vector.tensor_copy, QCOLS, 2 * QCOLS)
-        finish(0)
-        finish(1)
-        finish(2)
-        finish(3)
-        for q in range(4):
-            nc.scalar.dma_start(out_2[0, 4 * q : 4 * q + 4, :].bitcast(I32), o_scales[32 * q : 32 * q + 4, :].bitcast(I32))
+        for cols in quarters[2:]:
+            nc.scalar.copy(page_view[:, cols, LAST], pages[LAST][:, cols])
+        for cols in quarters[:2]:
+            nc.vector.tensor_copy(page_view[:, cols, LAST], pages[LAST][:, cols])
+        for group in (quarters[:2], quarters[2:3], quarters[3:]):
+            for cols in group:
+                quantize(o_codes[:, cols], o_scales[:, cols], page_bf[:, cols.start * PLANES : cols.stop * PLANES])
+            done = slice(group[0].start, group[-1].stop)
+            nc.sync.dma_start(words_out[:, done], o_codes[:, done].bitcast(I32))
+        for r in range(SCALE_ROWS):
+            nc.scalar.dma_start(out_2[0, r::SCALE_ROWS, :].bitcast(I32), o_scales[r:P:QUADRANT, :].bitcast(I32))

@@ -76,8 +76,7 @@ def tile_picked_momorderpagez_none_po_kernel(
         make_identity(nc, ident[:])
         pages = [sb("page%d" % t, [P, U], F32) for t in range(PLANES)]
         for t in range(PLANES):
-            engine = nc.vector if t < PLANES // 2 else nc.gpsimd
-            engine.memset(pages[t][:].bitcast(I32), 0)
+            nc.vector.memset(pages[t][:].bitcast(I32), 0)
 
         turned = turn.tile([P, P], F32, name="turned")
         nc.tensor.transpose(turned[:], g_rows[:], ident[:])

from contextlib import ExitStack

import concourse.mybir as mybir
from concourse.masks import make_identity

K, T, S, N, H, W, U = 512, 2048, 512, 512, 512, 256, 1024
FLOPS = 2 * K * S * H + 2 * K * S * N + 2 * S * H * N

F32 = mybir.dt.float32
BF16 = mybir.dt.bfloat16
I32 = mybir.dt.int32
U32 = mybir.dt.uint32
U16 = mybir.dt.uint16
U8 = mybir.dt.uint8
FP8X4 = mybir.dt.float8_e4m3fn_x4
ALU = mybir.AluOpType
ACT = mybir.ActivationFunctionType

P = 128
PLANES = 4
RUN = 8
QUADRANT = 32
SCALE_ROWS = 4
LINE = 4
HALVES = [slice(0, W), slice(W, 2 * W)]
QUARTER = U // 4
CV_SCALE = 0.0625
ORDER = (2, 0, 1, 3)
FIRST, LAST = ORDER[0], ORDER[-1]


def tile_picked_momorderpagez_none_po_kernel(
    tc, x_words, x_scales, wa, wb, gt, gi, offs, two, n1, n2, n3, n4, out_0, out_1, out_2
):
    nc = tc.nc
    with ExitStack() as ctx:
        keep = ctx.enter_context(tc.tile_pool(name="keep", bufs=1))
        banks = ctx.enter_context(tc.psum_pool(name="banks", bufs=7))
        turn = ctx.enter_context(tc.psum_pool(name="turn", bufs=1))

        def sb(name, shape, dtype, tag=None):
            return keep.tile(shape, dtype, name=name, tag=tag or name, align_bytes=64)

        def load_list(name, src):
            tile = sb(name, list(src.shape), U16)
            nc.sync.dma_start(tile[:], src)
            return tile

        xs = sb("xs", [P, T], U8)
        nc.vector.memset(xs[:].bitcast(I32), 0)
        l_offs = load_list("l_offs", offs)
        l_two = load_list("l_two", two)
        wa_raw = [sb("wa_raw%d" % h, [P, PLANES, W], F32) for h in range(2)]
        wa_rows = wa.rearrange("(p j) c -> p j c", j=PLANES)
        nc.sync.dma_start(wa_raw[0][:], wa_rows[:, :, HALVES[0]])
        for r in range(SCALE_ROWS):
            nc.sync.dma_start(xs[r:P:QUADRANT, :].bitcast(I32), x_scales[0, r::SCALE_ROWS, :].bitcast(I32))
        xw = sb("xw", [P, T], I32)
        nc.sync.dma_start(xw[:], x_words[0].rearrange("p c r -> p (c r)").bitcast(I32))
        g_rows = sb("g_rows", [P, P], F32, tag="g_rows_then_scales")
        nc.gpsimd.memset(g_rows[:], 0.0)
        for i, vec in enumerate((gt, gi)):
            nc.sync.dma_start(
                g_rows[PLANES * i : PLANES * (i + 1), :].rearrange("t (b j) -> t b j", j=RUN),
                vec.rearrange("(b t j) o -> t b (j o)", t=PLANES, j=RUN),
            )
        nc.sync.dma_start(wa_raw[1][:], wa_rows[:, :, HALVES[1]])
        l_n1 = load_list("l_n1", n1)
        l_n2 = load_list("l_n2", n2)
        wb_raw = sb("wb_raw", [P, PLANES, N], F32)
        nc.sync.dma_start(wb_raw[:], wb.rearrange("(p j) c -> p j c", j=PLANES))
        l_n4 = load_list("l_n4", n4)
        l_n3 = load_list("l_n3", n3)

        ident = sb("ident", [P, P], F32)
        make_identity(nc, ident[:])
        pages = [sb("page%d" % t, [P, U], F32) for t in range(PLANES)]
        for t in range(PLANES):
            nc.vector.memset(pages[t][:].bitcast(I32), 0)

        turned = turn.tile([P, P], F32, name="turned")
        nc.tensor.transpose(turned[:], g_rows[:], ident[:])
        gt_sign = sb("gt_sign", [P, PLANES], F32)
        g_cols = sb("g_cols", [P, 2 * PLANES], F32)
        gi_signed = sb("gi_signed", [P, PLANES], F32)
        nc.scalar.copy(g_cols[:], turned[:, 0 : 2 * PLANES])
        nc.gpsimd.tensor_scalar(gt_sign[:], g_cols[:, 0:PLANES], 0.0, 2.0, ALU.is_ge, ALU.mult)
        nc.gpsimd.tensor_scalar(gt_sign[:], gt_sign[:], 1.0, -1.0, ALU.mult, ALU.add)
        nc.gpsimd.tensor_tensor(gi_signed[:], g_cols[:, PLANES : 2 * PLANES], gt_sign[:], ALU.mult)

        def gather_words(name, lst, tag=None):
            words = sb(name, [P, S], U32, tag=tag)
            nc.vector.tensor_copy(
                words[:].rearrange("p (t b j) -> p b t j", t=PLANES, j=RUN), xw[:].bitcast(U32).indirect(lst[:])
            )
            return words

        def gather_bytes(name, lst):
            picked = sb(name, [P, S], U8)
            nc.vector.tensor_copy(picked[:], xs[:].indirect(lst[:]))
            return picked

        def deal_bytes(name, picked, tag=None):
            dealt = sb(name, [P, S], U8, tag=tag)
            nc.vector.tensor_copy(
                dealt[:].bitcast(I32).rearrange("p (t b w) -> p t b w", t=PLANES, w=2),
                picked[:].bitcast(I32).rearrange("p (b t w) -> p t b w", t=PLANES, w=2),
            )
            return dealt

        def round_weights(engine_copy, dst, raw):
            engine_copy(
                dst.rearrange("p (c i t) -> p c t i", i=LINE, t=PLANES), raw.rearrange("p t (c i) -> p c t i", i=LINE)
            )

        def quantize(codes, scales, src):
            nc.vector.quantize_mx(out=codes.bitcast(FP8X4), scales=scales, in_=src)

        def product(left_codes, left_scales, right_codes, right_scales, t, moving=slice(0, N)):
            bank = banks.tile([P, N], F32, name="bank")
            acc = bank[:, 0 : moving.stop - moving.start]
            fixed = slice(t * P, (t + 1) * P)
            nc.tensor.matmul_mx(
                out=acc, lhsT=left_codes[:, fixed].bitcast(FP8X4), lhsT_scale=left_scales[:, fixed],
                rhs=right_codes[:, moving].bitcast(FP8X4), rhs_scale=right_scales[:, moving], start=True, stop=True,
            )
            return acc

        xa_picked = gather_bytes("xa_picked", l_offs)
        xb_picked = gather_bytes("xb_picked", l_two)
        xb_scales = deal_bytes("xb_scales", xb_picked)

        gt_abs = sb("gt_abs", [P, PLANES], F32, tag="gt_wb_pairs")
        nc.scalar.activation(gt_abs[:], turned[:, 0:PLANES], ACT.Abs)

        wa_bf = [sb("wa_bf0", [P, W * PLANES], BF16), sb("wa_bf1", [P, W * PLANES], BF16, tag="wa_then_words")]
        wa_codes = sb("wa_codes", [P, H], U32)
        wa_scales = sb("wa_scales", [P, H], U8)

        def prepare_wa(h, engine_copy):
            round_weights(engine_copy, wa_bf[h][:], wa_raw[h][:])
            quantize(wa_codes[:, HALVES[h]], wa_scales[:, HALVES[h]], wa_bf[h][:])

        prepare_wa(0, nc.scalar.copy)
        xa_words = gather_words("xa_words", l_offs)
        xa_scales = deal_bytes("xa_scales", xa_picked, tag="g_rows_then_scales")
        prepare_wa(1, nc.vector.tensor_copy)
        xb_words = gather_words("xb_words", l_two, tag="wa_then_words")

        a = [sb("a%d" % t, [P, H], F32) for t in range(PLANES)]
        for t in range(PLANES):
            for cols in HALVES:
                acc = product(xa_words, xa_scales, wa_codes, wa_scales, t, cols)
                nc.scalar.activation(a[t][:, cols], acc, ACT.Copy, scale=gt_abs[:, t : t + 1])

        wb_bf = sb("wb_bf", [P, N * PLANES], BF16, tag="gt_wb_pairs")
        wb_codes = sb("wb_codes", [P, N], U32)
        wb_scales = sb("wb_scales", [P, N], U8)
        round_weights(nc.scalar.copy, wb_bf[:], wb_raw[:])

        pa = sb("pa", [P, PLANES * W], F32)
        pb = sb("pb", [P, PLANES * W], F32)
        for t in range(PLANES):
            nc.vector.tensor_copy(pa[:, t * W : (t + 1) * W], a[t][:].indirect(l_n1[:]))
            nc.vector.tensor_copy(pb[:, t * W : (t + 1) * W], a[t][:].indirect(l_n2[:]))
        quantize(wb_codes[:], wb_scales[:], wb_bf[:])
        pairs = sb("pairs", [P, 2 * PLANES * W], F32, tag="gt_wb_pairs")
        ra = pairs[:, 0 : PLANES * W]
        rb = pairs[:, PLANES * W : 2 * PLANES * W]
        nc.vector.tensor_tensor(ra, pa[:], pb[:], ALU.max)
        nc.vector.tensor_tensor(rb, pa[:], pb[:], ALU.min)

        z2_bf = [sb("z2_bf%d" % h, [P, W * PLANES], BF16, tag="z2_then_z%d" % h) for h in range(2)]
        for t in range(PLANES):
            acc = product(xb_words, xb_scales, wb_codes, wb_scales, t)
            for h in range(2):
                nc.scalar.activation(
                    z2_bf[h][:].rearrange("p (c t) -> p c t", t=PLANES)[:, :, t],
                    acc[:, HALVES[h]], ACT.Copy, scale=gi_signed[:, t : t + 1],
                )

        early, late = ORDER[:2], ORDER[2:]
        z = {t: sb("z%d" % t, [P, H], F32) for t in early}
        z_bf = sb("z_bf", [P, H * PLANES], BF16)
        z_view = z_bf[:].rearrange("p (u m t) -> p m u t", u=PLANES, t=PLANES)
        z_codes = sb("z_codes", [P, H], U32)
        z_scales = sb("z_scales", [P, H], U8)
        z2_codes = sb("z2_codes", [P, N], U32)
        z2_scales = sb("z2_scales", [P, N], U8)

        def put_larger(t):
            nc.vector.tensor_copy(z[t][:].indirect(l_n1[:]), ra[:, t * W : (t + 1) * W])

        def put_smaller(t):
            nc.vector.tensor_copy(z[t][:].indirect(l_n2[:]), rb[:, t * W : (t + 1) * W])

        def round_plane(view, t, src):
            lead = tuple(slice(None) for axis in src.shape)
            if t == FIRST:
                nc.scalar.copy(view[lead + (slice(FIRST, LAST + 1),)], src.unsqueeze(src.ndim).to_broadcast(list(src.shape) + [2]))
            else:
                nc.scalar.copy(view[lead + (t,)], src)

        def z_columns(t):
            return z[t][:].rearrange("p (m u) -> p m u", u=PLANES)

        for t in early:
            put_larger(t)
        for t in early:
            put_smaller(t)
            round_plane(z_view, t, z_columns(t))
        for h, t in enumerate(late):
            quantize(z2_codes[:, HALVES[h]], z2_scales[:, HALVES[h]], z2_bf[h][:])
            z[t] = sb("z%d" % t, [P, H], F32, tag="z2_then_z%d" % h)
        for t in late:
            put_larger(t)
        put_smaller(late[0])
        round_plane(z_view, late[0], z_columns(late[0]))
        put_smaller(LAST)

        def round_last_z(u):
            nc.vector.tensor_copy(z_view[:, :, u, LAST], z_columns(LAST)[:, :, u])

        def quantize_z(u):
            words = slice(u * P, (u + 1) * P)
            quantize(z_codes[:, words], z_scales[:, words], z_bf[:, u * P * PLANES : (u + 1) * P * PLANES])

        round_last_z(FIRST)
        for i, u in enumerate(ORDER):
            if u != LAST:
                round_last_z(ORDER[i + 1])
            quantize_z(u)

        cv = [sb("cv%d" % u, [P, N], F32) for u in range(PLANES)]
        pos = [sb("pos%d" % u, [P, N], F32) for u in range(PLANES)]
        neg = [sb("neg%d" % u, [P, N], F32) for u in range(PLANES)]
        pieces = {u: HALVES if u == FIRST else [slice(0, N)] for u in ORDER}
        accs = {u: [product(z_codes, z_scales, z2_codes, z2_scales, u, cols) for cols in pieces[u]] for u in ORDER}

        def empty(dst, u, func):
            for cols, acc in zip(pieces[u], accs[u]):
                nc.scalar.activation(dst[u][:, cols], acc, func, scale=CV_SCALE)

        empty(pos, FIRST, ACT.Relu)
        for i, u in enumerate(ORDER):
            if u != LAST:
                empty(pos, ORDER[i + 1], ACT.Relu)
            empty(cv, u, ACT.Copy)

        page_bf = sb("page_bf", [P, U * PLANES], BF16)
        page_view = page_bf[:].rearrange("p (c t) -> p c t", t=PLANES)
        out_rows = out_0.rearrange("(p t) c -> p t c", t=PLANES)

        def fetch(u):
            for h in range(2):
                entries = l_n4[:, h * (W // 16) : (h + 1) * (W // 16)]
                nc.vector.tensor_scalar(neg[u][:, HALVES[h]], pos[u][:].indirect(entries), -1.0, 0.0, ALU.mult, ALU.add)

        def put_page(u):
            nc.vector.tensor_tensor(pages[u][:].indirect(l_n3[:]), cv[u][:], neg[u][:], ALU.add)
            nc.sync.dma_start(out_rows[:, u, :], pages[u][:])

        fetch(FIRST)
        for i, u in enumerate(ORDER[:-1]):
            fetch(ORDER[i + 1])
            put_page(u)
            round_plane(page_view, u, pages[u][:])
        put_page(LAST)

        o_codes = sb("o_codes", [P, U], U32)
        o_scales = sb("o_scales", [P, U], U8)
        words_out = out_1[0].rearrange("p c r -> p (c r)").bitcast(I32)
        quarters = [slice(i * QUARTER, (i + 1) * QUARTER) for i in range(4)]

        for cols in quarters[2:]:
            nc.scalar.copy(page_view[:, cols, LAST], pages[LAST][:, cols])
        for cols in quarters[:2]:
            nc.vector.tensor_copy(page_view[:, cols, LAST], pages[LAST][:, cols])
        for group in (quarters[:2], quarters[2:3], quarters[3:]):
            for cols in group:
                quantize(o_codes[:, cols], o_scales[:, cols], page_bf[:, cols.start * PLANES : cols.stop * PLANES])
            done = slice(group[0].start, group[-1].stop)
            nc.sync.dma_start(words_out[:, done], o_codes[:, done].bitcast(I32))
        for r in range(SCALE_ROWS):
            nc.scalar.dma_start(out_2[0, r::SCALE_ROWS, :].bitcast(I32), o_scales[r:P:QUADRANT, :].bitcast(I32))
